import numpy as np
import ml_dtypes


def mxq(x, axis, fmt="e4m3"):
    dtype, down = {"e4m3": (ml_dtypes.float8_e4m3fn, 7), "e5m2": (ml_dtypes.float8_e5m2, 14)}[fmt]
    v = np.moveaxis(np.asarray(x, np.float32).astype(ml_dtypes.bfloat16).astype(np.float64), axis, -1)
    blocks = v.reshape(v.shape[:-1] + (-1, 32))
    amax = np.abs(blocks).max(-1, keepdims=True)
    byte = np.maximum(np.where(amax > 0, np.frexp(amax)[1] - 1 + 127, 0) - down, 1)
    scale = np.exp2(byte - 127.0)
    codes = (blocks / scale).astype(np.float32).astype(dtype).astype(np.float64)
    return np.moveaxis((codes * scale).reshape(v.shape), -1, axis)


WIDE = False


def mx_kscale(k):
    if not WIDE:
        return np.ones(k)
    levels = np.array([30, -30])
    if k % 512:
        return np.exp2(np.random.permutation(np.resize(levels, k // 32))).repeat(32)
    a = np.empty((k // 512, 16))
    for p in range(k // 512):
        a[p, :8] = np.random.permutation(np.resize(levels, 8))
        for g in range(8):
            far = levels[np.abs(levels - a[p, g]) >= 10]
            a[p, g + 8] = far[np.random.randint(len(far))]
    return np.exp2(a.ravel()).repeat(32)


def f64(x):
    return np.asarray(x).astype(np.float64)


def striped(idx):
    return np.tile(np.asarray(idx).reshape(-1, 16).T, (8, 1)).astype(np.uint16)


def unstriped(offs):
    return offs[:16].T.reshape(-1).astype(np.int64)


E2M1 = np.array([0.0, 0.5, 1.0, 1.5, 2.0, 3.0, 4.0, 6.0, -0.0, -0.5, -1.0, -1.5, -2.0, -3.0, -4.0, -6.0])


def pack_weight(w, fmt):
    k, n = w.shape
    w = f64(np.asarray(w, np.float32).astype(ml_dtypes.bfloat16)).reshape(k // 32, 32, n)
    amax = np.abs(w).max(1)
    if fmt == "e4m3":
        byte = np.frexp(amax)[1] - 1 + 127 - 7
    else:
        mant, ex = np.frexp(amax / 6.0)
        byte = np.where(mant > 0.5, ex, ex - 1) + 127
    byte = np.clip(np.where(amax > 0, byte, 1), 1, 254)
    scaled = (w * np.exp2(127.0 - byte)[:, None, :]).reshape(k, n).astype(np.float32)
    by_word = np.ascontiguousarray(scaled.reshape(k // 512, 128, 4, n).transpose(0, 1, 3, 2))
    if fmt == "e4m3":
        words = by_word.astype(ml_dtypes.float8_e4m3fn).view(np.uint8)
    else:
        c = by_word.astype(ml_dtypes.float4_e2m1fn).view(np.uint8) & 0xF
        words = (c[..., 0::2] | (c[..., 1::2] << 4)).reshape(k // 512, 128, 2 * n)
    return np.ascontiguousarray(words), np.ascontiguousarray(byte.astype(np.uint8).reshape(k // 512, 16, n))


def unpack_weight(words, scales, fmt):
    g, _, n = scales.shape
    words = np.ascontiguousarray(words).reshape(g, 128, n, -1)
    if fmt == "e4m3":
        vals = words.view(ml_dtypes.float8_e4m3fn).astype(np.float64)
    else:
        nib = np.empty((g, 128, n, 4), np.uint8)
        nib[..., 0::2] = words & 0xF
        nib[..., 1::2] = words >> 4
        vals = E2M1[nib]
    vals = vals * np.repeat(np.exp2(scales.astype(np.float64) - 127.0), 8, axis=1)[..., None]
    return vals.transpose(0, 1, 3, 2).reshape(g * 512, n)


K, T, Z, J, R, C, O, N, L, E = 512, 1024, 1024, 256, 512, 512, 256, 256, 512, 1024


def setup_inputs():
    n = np.random.standard_normal
    idx = np.random.permutation(T)[:J]
    idx2 = np.random.permutation(Z)[:J]
    idx3 = np.random.permutation(C)[:J]
    idx4 = np.random.permutation(C)[:J]
    idx5 = np.random.permutation(C)[:O]
    idx6 = np.random.permutation(C)[:O]
    idx7 = np.random.permutation(E)[:O]
    fk = mx_kscale(K)
    fr = mx_kscale(R)
    fl = mx_kscale(L)
    xtp = pack_weight(n((K, T)) / fk[:, None], "e2m1")
    xop = pack_weight(n((K, Z)) / fk[:, None], "e4m3")
    wp = pack_weight(n((K, R)) * 1 / np.sqrt(K) * fk[:, None] * fr, "e4m3")
    wbp = pack_weight(n((R, N)) * 1 / np.sqrt(R) / fr[:, None], "e2m1")
    sxp = pack_weight(n((L, O)) / fl[:, None], "e4m3")
    wsp = pack_weight(n((L, N)) * 1 / np.sqrt(L) * fl[:, None], "e4m3")
    return {
        "xt_words": xtp[0],
        "xt_scales": xtp[1],
        "xo_words": xop[0],
        "xo_scales": xop[1],
        "w_words": wp[0],
        "w_scales": wp[1],
        "wb_words": wbp[0],
        "wb_scales": wbp[1],
        "sx_words": sxp[0],
        "sx_scales": sxp[1],
        "ws_words": wsp[0],
        "ws_scales": wsp[1],
        "tz": (n((N, E))).astype(np.float32),
        "offs": striped(idx),
        "offs2": striped(idx2),
        "offs3": striped(idx3),
        "offs4": striped(idx4),
        "offs5": striped(idx5),
        "offs6": striped(idx6),
        "offs7": striped(idx7),
    }


def reference(xt_words, xt_scales, xo_words, xo_scales, w_words, w_scales, wb_words, wb_scales, sx_words, sx_scales, ws_words, ws_scales, tz, offs, offs2, offs3, offs4, offs5, offs6, offs7):
    idx = unstriped(offs)
    idx2 = unstriped(offs2)
    idx3 = unstriped(offs3)
    idx4 = unstriped(offs4)
    idx5 = unstriped(offs5)
    idx6 = unstriped(offs6)
    idx7 = unstriped(offs7)
    xtu = unpack_weight(xt_words, xt_scales, "e2m1")
    xou = unpack_weight(xo_words, xo_scales, "e4m3")
    wu = unpack_weight(w_words, w_scales, "e4m3")
    wbu = unpack_weight(wb_words, wb_scales, "e2m1")
    sxu = unpack_weight(sx_words, sx_scales, "e4m3")
    wsu = unpack_weight(ws_words, ws_scales, "e4m3")
    xtidxg = xtu[:, idx]
    a = wu.T @ xtidxg
    xoidx2g = xou[:, idx2]
    b = wu.T @ xoidx2g
    pw = np.zeros((R, C))
    pw[:, idx3] = a
    pv = np.zeros((R, C))
    pv[:, idx4] = b
    hid = np.abs(pw[:, idx5] - pv[:, idx6])
    hidq = mxq(hid, 0, "e5m2")
    p = wbu.T @ hidq + wsu.T @ sxu
    y = p + f64(tz)[:, idx7]
    return y

@@ -1,0 +1,231 @@
+from contextlib import ExitStack
+
+import concourse.mybir as mybir
+
+K, T, Z, J, R, C, O, N, L, E = 512, 1024, 1024, 256, 512, 512, 256, 256, 512, 1024
+FLOPS = 2 * (2 * K * R * J + R * N * O + L * N * O)
+
+P = 128
+PACK = 4
+HALF = O // 2
+
+F32 = mybir.dt.float32
+BF16 = mybir.dt.bfloat16
+I32 = mybir.dt.int32
+U32 = mybir.dt.uint32
+U16 = mybir.dt.uint16
+U8 = mybir.dt.uint8
+E4M3 = mybir.dt.float8_e4m3fn_x4
+E5M2 = mybir.dt.float8_e5m2_x4
+E2M1 = mybir.dt.float4_e2m1fn_x4
+ACT = mybir.ActivationFunctionType
+ALU = mybir.AluOpType
+
+
+def tile_list_oneforboth_twoboards_skip_tabled_kernel(
+    tc, xt_words, xt_scales, xo_words, xo_scales, w_words, w_scales, wb_words, wb_scales,
+    sx_words, sx_scales, ws_words, ws_scales, tz, offs, offs2, offs3, offs4, offs5, offs6, offs7, out,
+):
+    nc = tc.nc
+    with ExitStack() as ctx:
+        keep = ctx.enter_context(tc.tile_pool(name="keep", bufs=1))
+        shared = ctx.enter_context(tc.tile_pool(name="shared", bufs=1))
+        psum = ctx.enter_context(tc.psum_pool(name="psum", bufs=1))
+
+        def sb(name, shape, dtype, tag=None):
+            return keep.tile(shape, dtype, name=name, tag=tag or name, align_bytes=64)
+
+        def load_list(name, source):
+            held = keep.tile([P, J // 16], U16, name=name)
+            nc.sync.dma_start(held[:], source)
+            return held
+
+        def load_words(held, source):
+            flat = source[0] if source.ndim == 3 else source[0].rearrange("p n t -> p (n t)")
+            nc.sync.dma_start(held[:].bitcast(I32), flat.bitcast(I32))
+
+        def load_scale_rows(plane, source, quadrants):
+            for q in quadrants:
+                nc.sync.dma_start(
+                    plane[32 * q : 32 * q + 4, :].bitcast(I32), source[0, 4 * q : 4 * q + 4, :].bitcast(I32)
+                )
+
+        xt_plane = sb("xt_plane", [P, T], U8)
+        w_plane = sb("w_plane", [P, R], U8)
+        xo_plane = sb("xo_plane", [P, Z], U8)
+        wb_plane = sb("wb_plane", [P, N], U8)
+        ws_plane = sb("ws_plane", [P, N], U8)
+        sx_plane = sb("sx_plane", [P, O], U8)
+        nc.vector.memset(xt_plane[:, : T // 2].bitcast(I32), 0)
+        nc.gpsimd.memset(xt_plane[:, T // 2 :].bitcast(I32), 0)
+        nc.vector.memset(w_plane[:].bitcast(I32), 0)
+        nc.gpsimd.memset(xo_plane[:].bitcast(I32), 0)
+        pw = [sb(f"pw{t}", [P, C], F32) for t in range(PACK)]
+        pv = [sb(f"pv{t}", [P, C], F32) for t in range(PACK)]
+
+        xt_codes = sb("xt_codes", [P, T], U16)
+        xo_codes = sb("xo_codes", [P, Z], U32)
+        w_codes = sb("w_codes", [P, R], U32)
+        wb_codes = sb("wb_codes", [P, 2 * N], U8)
+        ws_codes = sb("ws_codes", [P, N], U32)
+        sx_codes = sb("sx_codes", [P, O], U32)
+
+        list1 = load_list("list1", offs)
+        load_scale_rows(xt_plane, xt_scales, range(4))
+        load_words(xt_codes, xt_words)
+        load_words(w_codes, w_words)
+        list3 = load_list("list3", offs3)
+        load_scale_rows(w_plane, w_scales, range(4))
+        list2 = load_list("list2", offs2)
+        load_words(xo_codes, xo_words)
+        load_scale_rows(xo_plane, xo_scales, range(4))
+        list4 = load_list("list4", offs4)
+        list5 = load_list("list5", offs5)
+        list6 = load_list("list6", offs6)
+        list7 = load_list("list7", offs7)
+        load_words(ws_codes, ws_words)
+        load_words(sx_codes, sx_words)
+        load_words(wb_codes, wb_words)
+
+        xt_picked = sb("xt_picked", [P, J], U16)
+        xt_picked_plane = sb("xt_picked_plane", [P, J], U8)
+        w_dealt = sb("w_dealt", [P, PACK, P], U32)
+        w_dealt_plane = sb("w_dealt_plane", [P, PACK, P], U8)
+
+        nc.vector.tensor_copy(xt_picked[:], xt_codes[:].indirect(list1[:]))
+        nc.vector.tensor_copy(xt_picked_plane[:], xt_plane[:].indirect(list1[:]))
+        nc.vector.tensor_copy(
+            w_dealt[:].bitcast(I32).rearrange("p t m -> p m t"),
+            w_codes[:].bitcast(I32).rearrange("p (m t) -> p m t", t=PACK),
+        )
+        for first, count in ((0, 1), (1, 1), (2, 2)):
+            nc.vector.tensor_copy(
+                w_dealt_plane[:, first : first + count, :],
+                w_plane[:].rearrange("p (m t) -> p t m", t=PACK)[:, first : first + count, :],
+            )
+
+        tz_rows = [sb(f"tz_rows{h}", [P, E], F32, ("xt_codes", "w_codes")[h]) for h in range(2)]
+        for h in range(2):
+            nc.sync.dma_start(tz_rows[h][:], tz[h * P : (h + 1) * P, :])
+        for board in pw[:2]:
+            nc.vector.memset(board[:].bitcast(I32), 0)
+        for board in pw[2:] + pv:
+            nc.gpsimd.memset(board[:].bitcast(I32), 0)
+        for plane, source in ((ws_plane, ws_scales), (sx_plane, sx_scales), (wb_plane, wb_scales)):
+            nc.vector.memset(plane[:].bitcast(I32), 0)
+            load_scale_rows(plane, source, range(4))
+
+        def first_stage(name, slices, moving, moving_plane):
+            bank = psum.tile([P, len(slices), J], F32, name=name)
+            for i, t in enumerate(slices):
+                nc.tensor.matmul_mx(
+                    out=bank[:, i, :], lhsT=w_dealt[:, t, :].bitcast(E4M3), lhsT_scale=w_dealt_plane[:, t, :],
+                    rhs=moving, rhs_scale=moving_plane, start=True, stop=True,
+                )
+            return bank
+
+        def copy_on(engine, dst, src):
+            if engine == "scalar":
+                nc.scalar.activation(dst, src, ACT.Copy)
+            else:
+                nc.vector.tensor_copy(dst, src)
+
+        def empty(engine, name, bank):
+            held = sb(name, list(bank.shape), F32)
+            copy_on(engine, held[:], bank[:])
+            return held
+
+        xt_operand = (xt_picked[:].bitcast(E2M1), xt_picked_plane[:])
+        bank_a0 = first_stage("bank_a0", [0], *xt_operand)
+        bank_a1 = first_stage("bank_a1", [1], *xt_operand)
+        bank_a23 = first_stage("bank_a23", [2, 3], *xt_operand)
+
+        diff = sb("diff", [P, PACK, O], F32)
+
+        def put(engine, board, offsets, values):
+            copy_on(engine, board[:].indirect(offsets[:]), values)
+
+        def read_pw(engine, t, held):
+            copy_on(engine, held, pw[t][:].indirect(list5[:]))
+            return held
+
+        def subtract(t, pw_read, first, count):
+            nc.vector.tensor_tensor(
+                diff[:, t, first : first + count],
+                pv[t][:].indirect(list6[:, first // 16 : (first + count) // 16]),
+                pw_read[:, first : first + count],
+                ALU.subtract,
+            )
+
+        a0 = empty("scalar", "a0", bank_a0)
+        a1 = shared.tile([P, 1, J], F32, name="a1", offset=512, align_bytes=64)
+        copy_on("vector", a1[:], bank_a1[:])
+        a23 = empty("scalar", "a23", bank_a23)
+        put("scalar", pw[0], list3, a0[:, 0, :])
+        put("vector", pw[1], list3, a1[:, 0, :])
+        xo_picked = shared.tile([P, J], U32, name="xo_picked", offset=0, align_bytes=64)
+        xo_picked_plane = shared.tile([P, J], U8, name="xo_picked_plane", offset=4 * J, align_bytes=64)
+        nc.vector.tensor_copy(xo_picked_plane[:], xo_plane[:].indirect(list2[:]))
+        nc.vector.tensor_copy(xo_picked[:], xo_codes[:].indirect(list2[:]))
+        xo_operand = (xo_picked[:].bitcast(E4M3), xo_picked_plane[:])
+        bank_b01 = first_stage("bank_b01", [0, 1], *xo_operand)
+        bank_b23 = first_stage("bank_b23", [2, 3], *xo_operand)
+        put("scalar", pw[2], list3, a23[:, 0, :])
+        put("scalar", pw[3], list3, a23[:, 1, :])
+        read01 = sb("read01", [P, 2 * O], F32, "xo_codes")
+        read1 = read_pw("vector", 1, read01[:, O:])
+        b01 = empty("vector", "b01", bank_b01)
+        b23 = empty("scalar", "b23", bank_b23)
+        read0 = read_pw("vector", 0, read01[:, :O])
+        read2 = read_pw("scalar", 2, sb("read2", [P, O], F32)[:])
+        put("vector", pv[0], list4, b01[:, 0, :])
+        put("vector", pv[1], list4, b01[:, 1, :])
+        put("scalar", pv[2], list4, b23[:, 0, :])
+        read3 = read_pw("scalar", 3, sb("read3", [P, O], F32)[:])
+        put("scalar", pv[3], list4, b23[:, 1, :])
+        subtract(0, read0, 0, O)
+        subtract(1, read1, 0, O)
+        for u in range(2):
+            subtract(2, read2, u * HALF, HALF)
+            subtract(3, read3, u * HALF, HALF)
+
+        banks = [psum.tile([P, 2, HALF], F32, name=f"bank_out{u}") for u in range(2)]
+        for u in range(2):
+            reads = slice(u * HALF, (u + 1) * HALF)
+            for h in range(2):
+                rows = slice(h * P, (h + 1) * P)
+                nc.tensor.matmul_mx(
+                    out=banks[u][:, h, :], lhsT=ws_codes[:, rows].bitcast(E4M3), lhsT_scale=ws_plane[:, rows],
+                    rhs=sx_codes[:, reads].bitcast(E4M3), rhs_scale=sx_plane[:, reads], start=(h == 0), stop=False,
+                )
+        tz_picked = [sb("tz_picked0", [P, O], F32, "b23")]
+        copy_on("scalar", tz_picked[0][:], tz_rows[0][:].indirect(list7[:]))
+
+        hid_all = sb("hid_all", [P, O * PACK], BF16, "xt_codes")
+        hid = [hid_all[:, u * HALF * PACK : (u + 1) * HALF * PACK] for u in range(2)]
+        hid_codes = [sb(f"hid_codes{u}", [P, HALF], U32) for u in range(2)]
+        hid_plane = [sb(f"hid_plane{u}", [P, HALF], U8) for u in range(2)]
+        result = [sb(f"result{u}", [P, 2, HALF], F32) for u in range(2)]
+        for u in range(2):
+            nc.scalar.activation(
+                hid[u].rearrange("p (c i t) -> p c t i", i=4, t=PACK),
+                diff[:, :, u * HALF : (u + 1) * HALF].rearrange("p t (c i) -> p c t i", i=4),
+                ACT.Abs,
+            )
+        tz_picked.append(sb("tz_picked1", [P, O], F32, "diff"))
+        copy_on("scalar", tz_picked[1][:], tz_rows[1][:].indirect(list7[:]))
+        for u in range(2):
+            nc.vector.quantize_mx(
+                out=hid_codes[u][:].bitcast(E5M2), scales=hid_plane[u][:], in_=hid[u]
+            )
+            for h in range(2):
+                nc.tensor.matmul_mx(
+                    out=banks[u][:, h, :], lhsT=wb_codes[:, 2 * h * P : 2 * (h + 1) * P].bitcast(E2M1),
+                    lhsT_scale=wb_plane[:, h * P : (h + 1) * P],
+                    rhs=hid_codes[u][:].bitcast(E5M2), rhs_scale=hid_plane[u][:], start=False, stop=(h == 1),
+                )
+        for u in range(2):
+            reads = slice(u * HALF, (u + 1) * HALF)
+            for h in range(2):
+                nc.vector.tensor_tensor(result[u][:, h, :], banks[u][:, h, :], tz_picked[h][:, reads], ALU.add)
+            nc.sync.dma_start(out.rearrange("(h p) o -> p h o", p=P)[:, :, reads], result[u][:])

@@ -29,7 +29,6 @@ def tile_list_oneforboth_twoboards_skip_tabled_kernel(
     nc = tc.nc
     with ExitStack() as ctx:
         keep = ctx.enter_context(tc.tile_pool(name="keep", bufs=1))
-        shared = ctx.enter_context(tc.tile_pool(name="shared", bufs=1))
         psum = ctx.enter_context(tc.psum_pool(name="psum", bufs=1))
 
         def sb(name, shape, dtype, tag=None):
@@ -89,6 +88,7 @@ def tile_list_oneforboth_twoboards_skip_tabled_kernel(
 
         xt_picked = sb("xt_picked", [P, J], U16)
         xt_picked_plane = sb("xt_picked_plane", [P, J], U8)
+        xo_picked_plane = sb("xo_picked_plane", [P, J], U8)
         w_dealt = sb("w_dealt", [P, PACK, P], U32)
         w_dealt_plane = sb("w_dealt_plane", [P, PACK, P], U8)
 
@@ -107,10 +107,8 @@ def tile_list_oneforboth_twoboards_skip_tabled_kernel(
         tz_rows = [sb(f"tz_rows{h}", [P, E], F32, ("xt_codes", "w_codes")[h]) for h in range(2)]
         for h in range(2):
             nc.sync.dma_start(tz_rows[h][:], tz[h * P : (h + 1) * P, :])
-        for board in pw[:2]:
+        for board in pw + pv:
             nc.vector.memset(board[:].bitcast(I32), 0)
-        for board in pw[2:] + pv:
-            nc.gpsimd.memset(board[:].bitcast(I32), 0)
         for plane, source in ((ws_plane, ws_scales), (sx_plane, sx_scales), (wb_plane, wb_scales)):
             nc.vector.memset(plane[:].bitcast(I32), 0)
             load_scale_rows(plane, source, range(4))
@@ -140,7 +138,7 @@ def tile_list_oneforboth_twoboards_skip_tabled_kernel(
         bank_a1 = first_stage("bank_a1", [1], *xt_operand)
         bank_a23 = first_stage("bank_a23", [2, 3], *xt_operand)
 
-        diff = sb("diff", [P, PACK, O], F32)
+        diff = [sb(f"diff{u}", [P, PACK, HALF], F32) for u in range(2)]
 
         def put(engine, board, offsets, values):
             copy_on(engine, board[:].indirect(offsets[:]), values)
@@ -149,22 +147,20 @@ def tile_list_oneforboth_twoboards_skip_tabled_kernel(
             copy_on(engine, held, pw[t][:].indirect(list5[:]))
             return held
 
-        def subtract(t, pw_read, first, count):
+        def subtract(t, pw_read, u):
             nc.vector.tensor_tensor(
-                diff[:, t, first : first + count],
-                pv[t][:].indirect(list6[:, first // 16 : (first + count) // 16]),
-                pw_read[:, first : first + count],
+                diff[u][:, t, :],
+                pv[t][:].indirect(list6[:, u * HALF // 16 : (u + 1) * HALF // 16]),
+                pw_read[:, u * HALF : (u + 1) * HALF],
                 ALU.subtract,
             )
 
         a0 = empty("scalar", "a0", bank_a0)
-        a1 = shared.tile([P, 1, J], F32, name="a1", offset=512, align_bytes=64)
-        copy_on("vector", a1[:], bank_a1[:])
+        a1 = empty("vector", "a1", bank_a1)
         a23 = empty("scalar", "a23", bank_a23)
         put("scalar", pw[0], list3, a0[:, 0, :])
         put("vector", pw[1], list3, a1[:, 0, :])
-        xo_picked = shared.tile([P, J], U32, name="xo_picked", offset=0, align_bytes=64)
-        xo_picked_plane = shared.tile([P, J], U8, name="xo_picked_plane", offset=4 * J, align_bytes=64)
+        xo_picked = sb("xo_picked", [P, J], U32, "a1")
         nc.vector.tensor_copy(xo_picked_plane[:], xo_plane[:].indirect(list2[:]))
         nc.vector.tensor_copy(xo_picked[:], xo_codes[:].indirect(list2[:]))
         xo_operand = (xo_picked[:].bitcast(E4M3), xo_picked_plane[:])
@@ -172,31 +168,34 @@ def tile_list_oneforboth_twoboards_skip_tabled_kernel(
         bank_b23 = first_stage("bank_b23", [2, 3], *xo_operand)
         put("scalar", pw[2], list3, a23[:, 0, :])
         put("scalar", pw[3], list3, a23[:, 1, :])
-        read01 = sb("read01", [P, 2 * O], F32, "xo_codes")
-        read1 = read_pw("vector", 1, read01[:, O:])
+        read0 = read_pw("scalar", 0, sb("read0", [P, O], F32)[:])
+        read1 = read_pw("vector", 1, sb("read1", [P, O], F32, "xo_codes")[:])
         b01 = empty("vector", "b01", bank_b01)
         b23 = empty("scalar", "b23", bank_b23)
-        read0 = read_pw("vector", 0, read01[:, :O])
         read2 = read_pw("scalar", 2, sb("read2", [P, O], F32)[:])
         put("vector", pv[0], list4, b01[:, 0, :])
         put("vector", pv[1], list4, b01[:, 1, :])
         put("scalar", pv[2], list4, b23[:, 0, :])
         read3 = read_pw("scalar", 3, sb("read3", [P, O], F32)[:])
         put("scalar", pv[3], list4, b23[:, 1, :])
-        subtract(0, read0, 0, O)
-        subtract(1, read1, 0, O)
+        for t, read in ((0, read0), (1, read1)):
+            for u in range(2):
+                subtract(t, read, u)
         for u in range(2):
-            subtract(2, read2, u * HALF, HALF)
-            subtract(3, read3, u * HALF, HALF)
+            subtract(2, read2, u)
+            subtract(3, read3, u)
 
-        banks = [psum.tile([P, 2, HALF], F32, name=f"bank_out{u}") for u in range(2)]
+        bank_tags = (("bank_a0", "bank_a1"), ("bank_out10", "bank_out11"))
+        banks = [
+            [psum.tile([P, HALF], F32, name=f"bank_out{u}{h}", tag=bank_tags[u][h]) for h in range(2)] for u in range(2)
+        ]
         for u in range(2):
             reads = slice(u * HALF, (u + 1) * HALF)
             for h in range(2):
                 rows = slice(h * P, (h + 1) * P)
                 nc.tensor.matmul_mx(
-                    out=banks[u][:, h, :], lhsT=ws_codes[:, rows].bitcast(E4M3), lhsT_scale=ws_plane[:, rows],
-                    rhs=sx_codes[:, reads].bitcast(E4M3), rhs_scale=sx_plane[:, reads], start=(h == 0), stop=False,
+                    out=banks[u][h][:], lhsT=ws_codes[:, rows].bitcast(E4M3), lhsT_scale=ws_plane[:, rows],
+                    rhs=sx_codes[:, reads].bitcast(E4M3), rhs_scale=sx_plane[:, reads], start=True, stop=False,
                 )
         tz_picked = [sb("tz_picked0", [P, O], F32, "b23")]
         copy_on("scalar", tz_picked[0][:], tz_rows[0][:].indirect(list7[:]))
@@ -205,14 +204,14 @@ def tile_list_oneforboth_twoboards_skip_tabled_kernel(
         hid = [hid_all[:, u * HALF * PACK : (u + 1) * HALF * PACK] for u in range(2)]
         hid_codes = [sb(f"hid_codes{u}", [P, HALF], U32) for u in range(2)]
         hid_plane = [sb(f"hid_plane{u}", [P, HALF], U8) for u in range(2)]
-        result = [sb(f"result{u}", [P, 2, HALF], F32) for u in range(2)]
+        result = [[sb(f"result{u}{h}", [P, HALF], F32) for h in range(2)] for u in range(2)]
         for u in range(2):
             nc.scalar.activation(
                 hid[u].rearrange("p (c i t) -> p c t i", i=4, t=PACK),
-                diff[:, :, u * HALF : (u + 1) * HALF].rearrange("p t (c i) -> p c t i", i=4),
+                diff[u][:].rearrange("p t (c i) -> p c t i", i=4),
                 ACT.Abs,
             )
-        tz_picked.append(sb("tz_picked1", [P, O], F32, "diff"))
+        tz_picked.append(sb("tz_picked1", [P, O], F32, "diff1"))
         copy_on("scalar", tz_picked[1][:], tz_rows[1][:].indirect(list7[:]))
         for u in range(2):
             nc.vector.quantize_mx(
@@ -220,12 +219,12 @@ def tile_list_oneforboth_twoboards_skip_tabled_kernel(
             )
             for h in range(2):
                 nc.tensor.matmul_mx(
-                    out=banks[u][:, h, :], lhsT=wb_codes[:, 2 * h * P : 2 * (h + 1) * P].bitcast(E2M1),
+                    out=banks[u][h][:], lhsT=wb_codes[:, 2 * h * P : 2 * (h + 1) * P].bitcast(E2M1),
                     lhsT_scale=wb_plane[:, h * P : (h + 1) * P],
-                    rhs=hid_codes[u][:].bitcast(E5M2), rhs_scale=hid_plane[u][:], start=False, stop=(h == 1),
+                    rhs=hid_codes[u][:].bitcast(E5M2), rhs_scale=hid_plane[u][:], start=False, stop=True,
                 )
         for u in range(2):
             reads = slice(u * HALF, (u + 1) * HALF)
             for h in range(2):
-                nc.vector.tensor_tensor(result[u][:, h, :], banks[u][:, h, :], tz_picked[h][:, reads], ALU.add)
-            nc.sync.dma_start(out.rearrange("(h p) o -> p h o", p=P)[:, :, reads], result[u][:])
+                nc.vector.tensor_tensor(result[u][h][:], banks[u][h][:], tz_picked[h][:, reads], ALU.add)
+                nc.sync.dma_start(out[h * P : (h + 1) * P, reads], result[u][h][:])

@@ -29,6 +29,7 @@ def tile_list_oneforboth_twoboards_skip_tabled_kernel(
     nc = tc.nc
     with ExitStack() as ctx:
         keep = ctx.enter_context(tc.tile_pool(name="keep", bufs=1))
+        shared = ctx.enter_context(tc.tile_pool(name="shared", bufs=1))
         psum = ctx.enter_context(tc.psum_pool(name="psum", bufs=1))
 
         def sb(name, shape, dtype, tag=None):
@@ -50,17 +51,15 @@ def tile_list_oneforboth_twoboards_skip_tabled_kernel(
                 )
 
         xt_plane = sb("xt_plane", [P, T], U8)
-        w_plane = sb("w_plane", [P, R], U8)
+        w_plane = shared.tile([P, R], U8, name="w_plane", offset=4 * C - R // 2, align_bytes=64)
         xo_plane = sb("xo_plane", [P, Z], U8)
         wb_plane = sb("wb_plane", [P, N], U8)
         ws_plane = sb("ws_plane", [P, N], U8)
         sx_plane = sb("sx_plane", [P, O], U8)
-        nc.vector.memset(xt_plane[:, : T // 2].bitcast(I32), 0)
-        nc.gpsimd.memset(xt_plane[:, T // 2 :].bitcast(I32), 0)
-        nc.vector.memset(w_plane[:].bitcast(I32), 0)
-        nc.gpsimd.memset(xo_plane[:].bitcast(I32), 0)
+        for plane in (xt_plane, w_plane, xo_plane):
+            nc.vector.memset(plane[:].bitcast(I32), 0)
         pw = [sb(f"pw{t}", [P, C], F32) for t in range(PACK)]
-        pv = [sb(f"pv{t}", [P, C], F32) for t in range(PACK)]
+        pv = [sb(f"pv{t}", [P, C], F32) for t in range(2)]
 
         xt_codes = sb("xt_codes", [P, T], U16)
         xo_codes = sb("xo_codes", [P, Z], U32)
@@ -112,6 +111,10 @@ def tile_list_oneforboth_twoboards_skip_tabled_kernel(
         for plane, source in ((ws_plane, ws_scales), (sx_plane, sx_scales), (wb_plane, wb_scales)):
             nc.vector.memset(plane[:].bitcast(I32), 0)
             load_scale_rows(plane, source, range(4))
+
+        for i in range(2):
+            pv.append(shared.tile([P, C], F32, name=f"pv{2 + i}", offset=4 * C * i, align_bytes=64))
+            nc.vector.memset(pv[2 + i][:].bitcast(I32), 0)
 
         def first_stage(name, slices, moving, moving_plane):
             bank = psum.tile([P, len(slices), J], F32, name=name)

@@ -171,10 +171,11 @@ def tile_list_oneforboth_twoboards_skip_tabled_kernel(
         bank_b23 = first_stage("bank_b23", [2, 3], *xo_operand)
         put("scalar", pw[2], list3, a23[:, 0, :])
         put("scalar", pw[3], list3, a23[:, 1, :])
-        read0 = read_pw("scalar", 0, sb("read0", [P, O], F32)[:])
-        read1 = read_pw("vector", 1, sb("read1", [P, O], F32, "xo_codes")[:])
+        read01 = sb("read01", [P, 2 * O], F32, "xo_codes")
+        read1 = read_pw("vector", 1, read01[:, O:])
         b01 = empty("vector", "b01", bank_b01)
         b23 = empty("scalar", "b23", bank_b23)
+        read0 = read_pw("vector", 0, read01[:, :O])
         read2 = read_pw("scalar", 2, sb("read2", [P, O], F32)[:])
         put("vector", pv[0], list4, b01[:, 0, :])
         put("vector", pv[1], list4, b01[:, 1, :])

from contextlib import ExitStack

import concourse.mybir as mybir

K, T, Z, J, R, C, O, N, L, E = 512, 1024, 1024, 256, 512, 512, 256, 256, 512, 1024
FLOPS = 2 * (2 * K * R * J + R * N * O + L * N * O)

P = 128
PACK = 4
HALF = O // 2

F32 = mybir.dt.float32
BF16 = mybir.dt.bfloat16
I32 = mybir.dt.int32
U32 = mybir.dt.uint32
U16 = mybir.dt.uint16
U8 = mybir.dt.uint8
E4M3 = mybir.dt.float8_e4m3fn_x4
E5M2 = mybir.dt.float8_e5m2_x4
E2M1 = mybir.dt.float4_e2m1fn_x4
ACT = mybir.ActivationFunctionType
ALU = mybir.AluOpType


def tile_list_oneforboth_twoboards_skip_tabled_kernel(
    tc, xt_words, xt_scales, xo_words, xo_scales, w_words, w_scales, wb_words, wb_scales,
    sx_words, sx_scales, ws_words, ws_scales, tz, offs, offs2, offs3, offs4, offs5, offs6, offs7, out,
):
    nc = tc.nc
    with ExitStack() as ctx:
        keep = ctx.enter_context(tc.tile_pool(name="keep", bufs=1))
        shared = ctx.enter_context(tc.tile_pool(name="shared", bufs=1))
        psum = ctx.enter_context(tc.psum_pool(name="psum", bufs=1))

        def sb(name, shape, dtype, tag=None):
            return keep.tile(shape, dtype, name=name, tag=tag or name, align_bytes=64)

        def load_list(name, source):
            held = keep.tile([P, J // 16], U16, name=name)
            nc.sync.dma_start(held[:], source)
            return held

        def load_words(held, source):
            flat = source[0] if source.ndim == 3 else source[0].rearrange("p n t -> p (n t)")
            nc.sync.dma_start(held[:].bitcast(I32), flat.bitcast(I32))

        def load_scale_rows(plane, source, quadrants):
            for q in quadrants:
                nc.sync.dma_start(
                    plane[32 * q : 32 * q + 4, :].bitcast(I32), source[0, 4 * q : 4 * q + 4, :].bitcast(I32)
                )

        xt_plane = sb("xt_plane", [P, T], U8)
        w_plane = shared.tile([P, R], U8, name="w_plane", offset=4 * C - R // 2, align_bytes=64)
        xo_plane = sb("xo_plane", [P, Z], U8)
        wb_plane = sb("wb_plane", [P, N], U8)
        ws_plane = sb("ws_plane", [P, N], U8)
        sx_plane = sb("sx_plane", [P, O], U8)
        for plane in (xt_plane, w_plane, xo_plane):
            nc.vector.memset(plane[:].bitcast(I32), 0)
        pw = [sb(f"pw{t}", [P, C], F32) for t in range(PACK)]
        pv = [sb(f"pv{t}", [P, C], F32) for t in range(2)]

        xt_codes = sb("xt_codes", [P, T], U16)
        xo_codes = sb("xo_codes", [P, Z], U32)
        w_codes = sb("w_codes", [P, R], U32)
        wb_codes = sb("wb_codes", [P, 2 * N], U8)
        ws_codes = sb("ws_codes", [P, N], U32)
        sx_codes = sb("sx_codes", [P, O], U32)

        list1 = load_list("list1", offs)
        load_scale_rows(xt_plane, xt_scales, range(4))
        load_words(xt_codes, xt_words)
        load_words(w_codes, w_words)
        list3 = load_list("list3", offs3)
        load_scale_rows(w_plane, w_scales, range(4))
        list2 = load_list("list2", offs2)
        load_words(xo_codes, xo_words)
        load_scale_rows(xo_plane, xo_scales, range(4))
        list4 = load_list("list4", offs4)
        list5 = load_list("list5", offs5)
        list6 = load_list("list6", offs6)
        list7 = load_list("list7", offs7)
        load_words(ws_codes, ws_words)
        load_words(sx_codes, sx_words)
        load_words(wb_codes, wb_words)

        xt_picked = sb("xt_picked", [P, J], U16)
        xt_picked_plane = sb("xt_picked_plane", [P, J], U8)
        xo_picked_plane = sb("xo_picked_plane", [P, J], U8)
        w_dealt = sb("w_dealt", [P, PACK, P], U32)
        w_dealt_plane = sb("w_dealt_plane", [P, PACK, P], U8)

        nc.vector.tensor_copy(xt_picked[:], xt_codes[:].indirect(list1[:]))
        nc.vector.tensor_copy(xt_picked_plane[:], xt_plane[:].indirect(list1[:]))
        nc.vector.tensor_copy(
            w_dealt[:].bitcast(I32).rearrange("p t m -> p m t"),
            w_codes[:].bitcast(I32).rearrange("p (m t) -> p m t", t=PACK),
        )
        for first, count in ((0, 1), (1, 1), (2, 2)):
            nc.vector.tensor_copy(
                w_dealt_plane[:, first : first + count, :],
                w_plane[:].rearrange("p (m t) -> p t m", t=PACK)[:, first : first + count, :],
            )

        tz_rows = [sb(f"tz_rows{h}", [P, E], F32, ("xt_codes", "w_codes")[h]) for h in range(2)]
        for h in range(2):
            nc.sync.dma_start(tz_rows[h][:], tz[h * P : (h + 1) * P, :])
        for board in pw + pv:
            nc.vector.memset(board[:].bitcast(I32), 0)
        for plane, source in ((ws_plane, ws_scales), (sx_plane, sx_scales), (wb_plane, wb_scales)):
            nc.vector.memset(plane[:].bitcast(I32), 0)
            load_scale_rows(plane, source, range(4))

        for i in range(2):
            pv.append(shared.tile([P, C], F32, name=f"pv{2 + i}", offset=4 * C * i, align_bytes=64))
            nc.vector.memset(pv[2 + i][:].bitcast(I32), 0)

        def first_stage(name, slices, moving, moving_plane):
            bank = psum.tile([P, len(slices), J], F32, name=name)
            for i, t in enumerate(slices):
                nc.tensor.matmul_mx(
                    out=bank[:, i, :], lhsT=w_dealt[:, t, :].bitcast(E4M3), lhsT_scale=w_dealt_plane[:, t, :],
                    rhs=moving, rhs_scale=moving_plane, start=True, stop=True,
                )
            return bank

        def copy_on(engine, dst, src):
            if engine == "scalar":
                nc.scalar.activation(dst, src, ACT.Copy)
            else:
                nc.vector.tensor_copy(dst, src)

        def empty(engine, name, bank):
            held = sb(name, list(bank.shape), F32)
            copy_on(engine, held[:], bank[:])
            return held

        xt_operand = (xt_picked[:].bitcast(E2M1), xt_picked_plane[:])
        bank_a0 = first_stage("bank_a0", [0], *xt_operand)
        bank_a1 = first_stage("bank_a1", [1], *xt_operand)
        bank_a23 = first_stage("bank_a23", [2, 3], *xt_operand)

        diff = [sb(f"diff{u}", [P, PACK, HALF], F32) for u in range(2)]

        def put(engine, board, offsets, values):
            copy_on(engine, board[:].indirect(offsets[:]), values)

        def read_pw(engine, t, held):
            copy_on(engine, held, pw[t][:].indirect(list5[:]))
            return held

        def subtract(t, pw_read, u):
            nc.vector.tensor_tensor(
                diff[u][:, t, :],
                pv[t][:].indirect(list6[:, u * HALF // 16 : (u + 1) * HALF // 16]),
                pw_read[:, u * HALF : (u + 1) * HALF],
                ALU.subtract,
            )

        a0 = empty("scalar", "a0", bank_a0)
        a1 = empty("vector", "a1", bank_a1)
        a23 = empty("scalar", "a23", bank_a23)
        put("scalar", pw[0], list3, a0[:, 0, :])
        put("vector", pw[1], list3, a1[:, 0, :])
        xo_picked = sb("xo_picked", [P, J], U32, "a1")
        nc.vector.tensor_copy(xo_picked_plane[:], xo_plane[:].indirect(list2[:]))
        nc.vector.tensor_copy(xo_picked[:], xo_codes[:].indirect(list2[:]))
        xo_operand = (xo_picked[:].bitcast(E4M3), xo_picked_plane[:])
        bank_b01 = first_stage("bank_b01", [0, 1], *xo_operand)
        bank_b23 = first_stage("bank_b23", [2, 3], *xo_operand)
        put("scalar", pw[2], list3, a23[:, 0, :])
        put("scalar", pw[3], list3, a23[:, 1, :])
        read01 = sb("read01", [P, 2 * O], F32, "xo_codes")
        read1 = read_pw("vector", 1, read01[:, O:])
        b01 = empty("vector", "b01", bank_b01)
        b23 = empty("scalar", "b23", bank_b23)
        read0 = read_pw("vector", 0, read01[:, :O])
        read2 = read_pw("scalar", 2, sb("read2", [P, O], F32)[:])
        put("vector", pv[0], list4, b01[:, 0, :])
        put("vector", pv[1], list4, b01[:, 1, :])
        put("scalar", pv[2], list4, b23[:, 0, :])
        read3 = read_pw("scalar", 3, sb("read3", [P, O], F32)[:])
        put("scalar", pv[3], list4, b23[:, 1, :])
        for t, read in ((0, read0), (1, read1)):
            for u in range(2):
                subtract(t, read, u)
        for u in range(2):
            subtract(2, read2, u)
            subtract(3, read3, u)

        bank_tags = (("bank_a0", "bank_a1"), ("bank_out10", "bank_out11"))
        banks = [
            [psum.tile([P, HALF], F32, name=f"bank_out{u}{h}", tag=bank_tags[u][h]) for h in range(2)] for u in range(2)
        ]
        for u in range(2):
            reads = slice(u * HALF, (u + 1) * HALF)
            for h in range(2):
                rows = slice(h * P, (h + 1) * P)
                nc.tensor.matmul_mx(
                    out=banks[u][h][:], lhsT=ws_codes[:, rows].bitcast(E4M3), lhsT_scale=ws_plane[:, rows],
                    rhs=sx_codes[:, reads].bitcast(E4M3), rhs_scale=sx_plane[:, reads], start=True, stop=False,
                )
        tz_picked = [sb("tz_picked0", [P, O], F32, "b23")]
        copy_on("scalar", tz_picked[0][:], tz_rows[0][:].indirect(list7[:]))

        hid_all = sb("hid_all", [P, O * PACK], BF16, "xt_codes")
        hid = [hid_all[:, u * HALF * PACK : (u + 1) * HALF * PACK] for u in range(2)]
        hid_codes = [sb(f"hid_codes{u}", [P, HALF], U32) for u in range(2)]
        hid_plane = [sb(f"hid_plane{u}", [P, HALF], U8) for u in range(2)]
        result = [[sb(f"result{u}{h}", [P, HALF], F32) for h in range(2)] for u in range(2)]
        for u in range(2):
            nc.scalar.activation(
                hid[u].rearrange("p (c i t) -> p c t i", i=4, t=PACK),
                diff[u][:].rearrange("p t (c i) -> p c t i", i=4),
                ACT.Abs,
            )
        tz_picked.append(sb("tz_picked1", [P, O], F32, "diff1"))
        copy_on("scalar", tz_picked[1][:], tz_rows[1][:].indirect(list7[:]))
        for u in range(2):
            nc.vector.quantize_mx(
                out=hid_codes[u][:].bitcast(E5M2), scales=hid_plane[u][:], in_=hid[u]
            )
            for h in range(2):
                nc.tensor.matmul_mx(
                    out=banks[u][h][:], lhsT=wb_codes[:, 2 * h * P : 2 * (h + 1) * P].bitcast(E2M1),
                    lhsT_scale=wb_plane[:, h * P : (h + 1) * P],
                    rhs=hid_codes[u][:].bitcast(E5M2), rhs_scale=hid_plane[u][:], start=False, stop=True,
                )
        for u in range(2):
            reads = slice(u * HALF, (u + 1) * HALF)
            for h in range(2):
                nc.vector.tensor_tensor(result[u][h][:], banks[u][h][:], tz_picked[h][:, reads], ALU.add)
                nc.sync.dma_start(out[h * P : (h + 1) * P, reads], result[u][h][:])
